import numpy as np
import ml_dtypes


def mxq(x, axis, fmt="e4m3"):
    dtype, down = {"e4m3": (ml_dtypes.float8_e4m3fn, 7), "e5m2": (ml_dtypes.float8_e5m2, 14)}[fmt]
    v = np.moveaxis(np.asarray(x, np.float32).astype(ml_dtypes.bfloat16).astype(np.float64), axis, -1)
    blocks = v.reshape(v.shape[:-1] + (-1, 32))
    amax = np.abs(blocks).max(-1, keepdims=True)
    byte = np.maximum(np.where(amax > 0, np.frexp(amax)[1] - 1 + 127, 0) - down, 1)
    scale = np.exp2(byte - 127.0)
    codes = (blocks / scale).astype(np.float32).astype(dtype).astype(np.float64)
    return np.moveaxis((codes * scale).reshape(v.shape), -1, axis)


WIDE = False


def mx_kscale(k, group=512):
    if not WIDE:
        return np.ones(k)
    levels = np.array([10, -10, 5, -5, 0])
    if group != 512:
        return np.exp2(np.random.permutation(np.resize(levels, k // group))).repeat(group)
    if k % 512:
        return np.exp2(np.random.permutation(np.resize(levels, k // 32))).repeat(32)
    a = np.empty((k // 512, 16))
    for p in range(k // 512):
        a[p, :8] = np.random.permutation(np.resize(levels, 8))
        for g in range(8):
            far = levels[np.abs(levels - a[p, g]) >= 10]
            a[p, g + 8] = far[np.random.randint(len(far))]
    return np.exp2(a.ravel()).repeat(32)


def f64(x):
    return np.asarray(x).astype(np.float64)


def sigmoid(v):
    return 1.0 / (1.0 + np.exp(-v))


G, D, M, O, N = 2, 256, 128, 256, 512


def setup_inputs():
    n = np.random.standard_normal
    s_d = mx_kscale(D, 0)
    s_o = mx_kscale(O, 0)
    return {
        "x": (n((G, D, N)) * s_d[:, None]).astype(np.float32),
        "w1": (n((G, D, M)) / np.sqrt(D) / s_d[:, None]).astype(np.float32),
        "w2": (n((G, D, M)) / np.sqrt(D) / s_d[:, None]).astype(np.float32),
        "st": (np.random.uniform(4.0, 16.0, (G, M, 1))).astype(np.float32),
        "gb": (0.5 * n((G, M, 1))).astype(np.float32),
        "wo": (n((G, O, M)) / np.sqrt(O) / s_o[:, None]).astype(np.float32),
        "dy": (n((G, O, N)) * s_o[:, None]).astype(np.float32),
        "og": (np.random.uniform(0.3, 1.0, (G, M, 1))).astype(np.float32),
        "base": (0.2 * n((G, M, N))).astype(np.float32),
    }


def reference(x, w1, w2, st, gb, wo, dy, og, base):
    w1q = mxq(f64(w1), 1, "e4m3")
    xq = mxq(f64(x), 1, "e4m3")
    z1 = w1q.transpose(0, 2, 1) @ xq
    w2q = mxq(f64(w2), 1, "e4m3")
    z2 = w2q.transpose(0, 2, 1) @ xq
    mu = np.mean(z1 * z2, axis=-1, keepdims=True)
    gt = sigmoid(mu * f64(st) + f64(gb))
    woq = mxq(f64(wo), 1, "e4m3")
    dyq = mxq(f64(dy), 1, "e4m3")
    c0 = woq.transpose(0, 2, 1) @ dyq
    dgt = np.sum(c0 * z1, axis=-1, keepdims=True)
    dmu = dgt * gt * (1.0 - gt) * f64(st)
    dz1 = c0 * gt + dmu / 512.0 * z2
    kdz1 = dz1 * 2.0
    kdmu = np.sum(kdz1 * z2, axis=-1, keepdims=True) / 512.0
    kdgt = kdmu * f64(st) * (1.0 - gt) * gt
    kgt = np.sum(kdz1 * c0, axis=-1, keepdims=True) + kdmu * f64(st) * (1.0 - gt) * dgt - kdmu * f64(st) * dgt * gt
    kmu = kgt * gt * (1.0 - gt) * f64(st)
    kz1 = kdgt * c0 + kmu / 512.0 * z2
    y = kz1 * f64(og) + f64(base)
    return y

@@ -1,0 +1,217 @@
+from contextlib import ExitStack
+
+import concourse.mybir as mybir
+
+G, D, M, N = 2, 256, 128, 512
+FLOPS = 3 * 2 * G * D * M * N
+
+F32 = mybir.dt.float32
+BF16 = mybir.dt.bfloat16
+U32 = mybir.dt.uint32
+U8 = mybir.dt.uint8
+FP8X4 = mybir.dt.float8_e4m3fn_x4
+ALU = mybir.AluOpType
+ACT = mybir.ActivationFunctionType
+
+P = 128
+PACK = 4
+ROWS = D // PACK
+HALF = N // 2
+MM_N = 128
+RUN = 4
+XA_V, XB_V, DYA_V, DYB_V = 160, 160, 192, 160
+
+
+def tile_rows_gprowgate_kernel(tc, x, w1, w2, st, gb, wo, dy, og, base, out):
+    nc = tc.nc
+    with ExitStack() as ctx:
+        sb = ctx.enter_context(tc.tile_pool(name="sb", bufs=1))
+        ps = ctx.enter_context(tc.psum_pool(name="ps", bufs=1))
+        ctx.enter_context(tc.manual_schedule())
+
+        def load(name, src, lo, hi):
+            raw = sb.tile([P, PACK, hi - lo], F32, name=name, align_bytes=64)
+            nc.sync.dma_start(out=raw[:], in_=src.rearrange("g (p j) n -> (g p) j n", j=PACK)[:, :, lo:hi])
+            return raw
+
+        def operand(name, width):
+            grouped = sb.tile([P, width, PACK], BF16, name=name + "_bf", align_bytes=64)
+            codes = sb.tile([P, width], U32, name=name + "_codes", align_bytes=64)
+            scales = sb.tile([P, width], U8, name=name + "_scales", align_bytes=64)
+            return grouped, codes, scales
+
+        def interleave(copy, op, at, raw, lo, hi):
+            copy(
+                out=op[0][:, at + lo : at + hi, :].rearrange("p (c i) j -> p c j i", i=RUN),
+                in_=raw[:, :, lo:hi].rearrange("p j (c i) -> p c j i", i=RUN),
+            )
+
+        def quantize(op):
+            nc.vector.quantize_mx(
+                out=op[1][:].bitcast(FP8X4), scales=op[2][:], in_=op[0][:].rearrange("p w j -> p (w j)")
+            )
+
+        def product(banks, at, weights, w_at, moving):
+            for c in range(0, HALF, MM_N):
+                for g in range(G):
+                    rows = slice(g * ROWS, (g + 1) * ROWS)
+                    nc.tensor.matmul_mx(
+                        out=banks[g][:, at + c : at + c + MM_N],
+                        lhsT=weights[1][rows, w_at : w_at + M].bitcast(FP8X4),
+                        lhsT_scale=weights[2][rows, w_at : w_at + M],
+                        rhs=moving[1][rows, c : c + MM_N].bitcast(FP8X4),
+                        rhs_scale=moving[2][rows, c : c + MM_N],
+                        start=True,
+                        stop=True,
+                    )
+
+        def small(name, *shape):
+            return sb.tile([P, *shape], F32, name=name)
+
+        def cross_sum(name, left, right, factor):
+            total = small(name, 1)
+            terms = small(name + "_terms", N)
+            nc.vector.scalar_tensor_tensor(
+                out=terms[:], in0=left, scalar=factor, in1=right, op0=ALU.mult, op1=ALU.mult, accum_out=total[:]
+            )
+            return total
+
+        def square_sum(name, values):
+            total = small(name, 1)
+            terms = small(name + "_terms", N)
+            nc.scalar.activation(out=terms[:], in_=values, func=ACT.Square, scale=1.0 / 32.0, accum_out=total[:])
+            return total
+
+        def affine(result, value, scale, bias=0.0):
+            nc.scalar.activation(out=result, in_=value, func=ACT.Identity, scale=scale, bias=bias)
+
+        def fused(result, in0, number, op0, in1):
+            nc.vector.scalar_tensor_tensor(out=result, in0=in0, scalar=number, in1=in1, op0=op0, op1=ALU.mult)
+
+        vec_rows = sb.tile([P, P], F32, name="vec_rows", align_bytes=64)
+        vec_cols = sb.tile([P, P], F32, name="vec_cols", align_bytes=64)
+        nc.vector.memset(vec_rows[:], 0.0)
+        by_group = vec_cols[:].rearrange("p (g k) -> p g k", k=32)
+        st_c, gb_c, og_c = by_group[:, 0:G, 0], by_group[:, 0:G, 1], by_group[:, 0:G, 2]
+
+        w1_raw = load("w1_raw", w1, 0, M)
+        w2_raw = load("w2_raw", w2, 0, M)
+        xa_raw = load("xa_raw", x, 0, HALF)
+        for k, vec in enumerate((st, gb, og)):
+            nc.sync.dma_start(
+                out=vec_rows[k:P:32, 0 : G * 32].rearrange("q (g i) -> q g i", g=G),
+                in_=vec.rearrange("g (q i) o -> q g (i o)", i=32),
+            )
+        xb_raw = load("xb_raw", x, HALF, N)
+        wo_raw = load("wo_raw", wo, 0, M)
+        dya_raw = load("dya_raw", dy, 0, HALF)
+        dyb_raw = load("dyb_raw", dy, HALF, N)
+        base_sb = small("base_sb", G, N)
+        nc.sync.dma_start(out=base_sb[:], in_=base.rearrange("g m n -> m g n"))
+
+        w12 = operand("w12", 2 * M)
+        wo_q = operand("wo_q", M)
+        xa, xb, dya, dyb = [operand(name, HALF) for name in ("xa", "xb", "dya", "dyb")]
+        z_ps = [[ps.tile([P, N], F32, name="z_ps%d%d" % (h, g)) for g in range(G)] for h in range(2)]
+        c_ps = [ps.tile([P, N], F32, name="c_ps%d" % g) for g in range(G)]
+        c_twin = [ps.tile([P, N], F32, name="c_twin%d" % g) for g in range(G)]
+        z_sb = [small("z_sb%d" % g, 2, N) for g in range(G)]
+        vcopy, scopy = nc.vector.tensor_copy, nc.scalar.copy
+
+        def z_out(copy, h, g):
+            copy(out=z_sb[g][:, :, h * HALF : (h + 1) * HALF], in_=z_ps[h][g][:].rearrange("p (k n) -> p k n", k=2))
+
+        interleave(vcopy, w12, 0, w1_raw, 0, M)
+        interleave(vcopy, w12, M, w2_raw, 0, M)
+        quantize(w12)
+
+        interleave(vcopy, xa, 0, xa_raw, 0, XA_V)
+        interleave(scopy, xa, 0, xa_raw, XA_V, HALF)
+        nc.vector.transpose(out=vec_cols[:], in_=vec_rows[:])
+        quantize(xa)
+        product(z_ps[0], 0, w12, 0, xa)
+        product(z_ps[0], HALF, w12, M, xa)
+
+        t_st = small("t_st", G, 2)
+        consts = small("consts", G, 3)
+        gb_half = small("gb_half", G)
+        interleave(vcopy, xb, 0, xb_raw, 0, XB_V)
+        interleave(scopy, xb, 0, xb_raw, XB_V, HALF)
+        fused(consts[:, :, 2], st_c, 0.5, ALU.mult, og_c)
+        nc.vector.tensor_scalar(out=gb_half[:], in0=gb_c, scalar1=0.5, scalar2=None, op0=ALU.mult)
+        nc.vector.tensor_copy(out=consts[:, :, 0], in_=st_c)
+        nc.vector.tensor_copy(out=t_st[:, :, 1], in_=st_c)
+        quantize(xb)
+        product(z_ps[1], 0, w12, 0, xb)
+        product(z_ps[1], HALF, w12, M, xb)
+
+        interleave(scopy, wo_q, 0, wo_raw, 0, M)
+        z_out(vcopy, 0, 1)
+        z_out(scopy, 0, 0)
+        quantize(wo_q)
+
+        interleave(vcopy, dya, 0, dya_raw, 0, DYA_V)
+        interleave(scopy, dya, 0, dya_raw, DYA_V, HALF)
+        quantize(dya)
+        product(c_ps, 0, wo_q, 0, dya)
+        product(c_twin, 0, wo_q, 0, dya)
+        z_out(scopy, 1, 0)
+
+        interleave(vcopy, dyb, 0, dyb_raw, 0, DYB_V)
+        interleave(scopy, dyb, 0, dyb_raw, DYB_V, HALF)
+        z_out(scopy, 1, 1)
+        quantize(dyb)
+        product(c_ps, HALF, wo_q, 0, dyb)
+        product(c_twin, HALF, wo_q, 0, dyb)
+
+        s12 = [cross_sum("s12_%d" % g, z_sb[g][:, 0, :], z_sb[g][:, 1, :], 0.5 / N) for g in range(G)]
+        s22 = [square_sum("s22_%d" % g, z_sb[g][:, 1, :]) for g in range(G)]
+        for g in range(G):
+            nc.scalar.activation(
+                out=t_st[:, g, 0:1], in_=s12[g][:], func=ACT.Tanh, scale=t_st[:, g, 1:2], bias=gb_half[:, g : g + 1]
+            )
+        for g in range(G):
+            affine(consts[:, g, 1:2], s22[g][:], t_st[:, g, 1:2])
+        scc = [square_sum("scc_%d" % g, c_twin[g][:]) for g in range(G)]
+
+        u_r = small("u_r", G, 2)
+        slopes = small("slopes", G, 3)
+        coef = small("coef", G, 3)
+        p0 = cross_sum("p0", c_ps[0][:], z_sb[0][:, 1, :], 0.5 / N)
+        fused(u_r[:], t_st[:, :, 0:1].to_broadcast([P, G, 2]), -1.0, ALU.mult, t_st[:])
+        d0 = cross_sum("d0", c_ps[0][:], z_sb[0][:, 0, :], 1.0 / N)
+        fused(slopes[:], u_r[:, :, 0:1].to_broadcast([P, G, 3]), 1.0, ALU.add, consts[:])
+        p1 = cross_sum("p1", c_ps[1][:], z_sb[1][:, 1, :], 0.5 / N)
+        fused(coef[:, :, 0], t_st[:, :, 0], 1.0, ALU.add, slopes[:, :, 2])
+        fused(coef[:, :, 1:3], slopes[:, :, 0:2], 0.5, ALU.mult, slopes[:, :, 2:3].to_broadcast([P, G, 2]))
+        d1 = cross_sum("d1", c_ps[1][:], z_sb[1][:, 0, :], 1.0 / N)
+        p_sum, d_sum = [p0, p1], [d0, d1]
+
+        from_p = [small("from_p%d" % g, 2) for g in range(G)]
+        from_s = [small("from_s%d" % g, 1) for g in range(G)]
+        a_c = [small("a_c%d" % g, 1) for g in range(G)]
+        inner = [small("inner%d" % g, 1) for g in range(G)]
+        b_c = [small("b_c%d" % g, 1) for g in range(G)]
+        for g in range(G):
+            affine(from_p[g][:], coef[:, g, 0:2], p_sum[g][:])
+        affine(a_c[0][:], d_sum[0][:], coef[:, 0, 2:3], from_p[0][:, 0:1])
+        for g in range(G):
+            affine(from_s[g][:], scc[g][:], coef[:, g, 0:1])
+        affine(inner[0][:], a_c[0][:], u_r[:, 0, 1:2], from_p[0][:, 1:2])
+        affine(a_c[1][:], d_sum[1][:], coef[:, 1, 2:3], from_p[1][:, 0:1])
+        affine(b_c[0][:], inner[0][:], d_sum[0][:], from_s[0][:])
+        affine(inner[1][:], a_c[1][:], u_r[:, 1, 1:2], from_p[1][:, 1:2])
+        affine(b_c[1][:], inner[1][:], d_sum[1][:], from_s[1][:])
+
+        part = [small("part%d" % g, N) for g in range(G)]
+        result = [small("result%d" % g, N) for g in range(G)]
+        for g in range(G):
+            nc.vector.scalar_tensor_tensor(
+                out=part[g][:], in0=c_ps[g][:], scalar=a_c[g][:], in1=base_sb[:, g, :], op0=ALU.mult, op1=ALU.add
+            )
+        for g, cols in ((0, slice(0, N)), (1, slice(0, HALF)), (1, slice(HALF, N))):
+            nc.vector.scalar_tensor_tensor(
+                out=result[g][:, cols], in0=z_sb[g][:, 1, cols], scalar=b_c[g][:], in1=part[g][:, cols],
+                op0=ALU.mult, op1=ALU.add,
+            )
+            nc.sync.dma_start(out=out[g, :, cols], in_=result[g][:, cols])

@@ -17,9 +17,9 @@ P = 128
 PACK = 4
 ROWS = D // PACK
 HALF = N // 2
-MM_N = 128
 RUN = 4
-XA_V, XB_V, DYA_V, DYB_V = 160, 160, 192, 160
+X_V = 192
+DY_V = 176
 
 
 def tile_rows_gprowgate_kernel(tc, x, w1, w2, st, gb, wo, dy, og, base, out):
@@ -29,9 +29,12 @@ def tile_rows_gprowgate_kernel(tc, x, w1, w2, st, gb, wo, dy, og, base, out):
         ps = ctx.enter_context(tc.psum_pool(name="ps", bufs=1))
         ctx.enter_context(tc.manual_schedule())
 
-        def load(name, src, lo, hi):
-            raw = sb.tile([P, PACK, hi - lo], F32, name=name, align_bytes=64)
-            nc.sync.dma_start(out=raw[:], in_=src.rearrange("g (p j) n -> (g p) j n", j=PACK)[:, :, lo:hi])
+        def small(name, *shape):
+            return sb.tile([P, *shape], F32, name=name)
+
+        def load(name, src):
+            raw = sb.tile([P, PACK, src.shape[2]], F32, name=name, align_bytes=64)
+            nc.sync.dma_start(out=raw[:], in_=src.rearrange("g (p j) n -> (g p) j n", j=PACK))
             return raw
 
         def operand(name, width):
@@ -40,33 +43,31 @@ def tile_rows_gprowgate_kernel(tc, x, w1, w2, st, gb, wo, dy, og, base, out):
             scales = sb.tile([P, width], U8, name=name + "_scales", align_bytes=64)
             return grouped, codes, scales
 
-        def interleave(copy, op, at, raw, lo, hi):
+        def interleave(copy, op, raw, lo, hi):
             copy(
-                out=op[0][:, at + lo : at + hi, :].rearrange("p (c i) j -> p c j i", i=RUN),
+                out=op[0][:, lo:hi, :].rearrange("p (c i) j -> p c j i", i=RUN),
                 in_=raw[:, :, lo:hi].rearrange("p j (c i) -> p c j i", i=RUN),
             )
 
-        def quantize(op):
+        def quantize(op, lo, hi):
             nc.vector.quantize_mx(
-                out=op[1][:].bitcast(FP8X4), scales=op[2][:], in_=op[0][:].rearrange("p w j -> p (w j)")
+                out=op[1][:, lo:hi].bitcast(FP8X4),
+                scales=op[2][:, lo:hi],
+                in_=op[0][:, lo:hi, :].rearrange("p w j -> p (w j)"),
             )
 
-        def product(banks, at, weights, w_at, moving):
-            for c in range(0, HALF, MM_N):
-                for g in range(G):
-                    rows = slice(g * ROWS, (g + 1) * ROWS)
-                    nc.tensor.matmul_mx(
-                        out=banks[g][:, at + c : at + c + MM_N],
-                        lhsT=weights[1][rows, w_at : w_at + M].bitcast(FP8X4),
-                        lhsT_scale=weights[2][rows, w_at : w_at + M],
-                        rhs=moving[1][rows, c : c + MM_N].bitcast(FP8X4),
-                        rhs_scale=moving[2][rows, c : c + MM_N],
-                        start=True,
-                        stop=True,
-                    )
-
-        def small(name, *shape):
-            return sb.tile([P, *shape], F32, name=name)
+        def product(banks, weights, moving):
+            for g in range(len(banks)):
+                rows = slice(g * ROWS, (g + 1) * ROWS)
+                nc.tensor.matmul_mx(
+                    out=banks[g][:],
+                    lhsT=weights[1][rows, :].bitcast(FP8X4),
+                    lhsT_scale=weights[2][rows, :],
+                    rhs=moving[1][rows, :].bitcast(FP8X4),
+                    rhs_scale=moving[2][rows, :],
+                    start=True,
+                    stop=True,
+                )
 
         def cross_sum(name, left, right, factor):
             total = small(name, 1)
@@ -94,124 +95,129 @@ def tile_rows_gprowgate_kernel(tc, x, w1, w2, st, gb, wo, dy, og, base, out):
         by_group = vec_cols[:].rearrange("p (g k) -> p g k", k=32)
         st_c, gb_c, og_c = by_group[:, 0:G, 0], by_group[:, 0:G, 1], by_group[:, 0:G, 2]
 
-        w1_raw = load("w1_raw", w1, 0, M)
-        w2_raw = load("w2_raw", w2, 0, M)
-        xa_raw = load("xa_raw", x, 0, HALF)
+        x_raw = load("x_raw", x)
+        w1_raw = load("w1_raw", w1)
         for k, vec in enumerate((st, gb, og)):
             nc.sync.dma_start(
                 out=vec_rows[k:P:32, 0 : G * 32].rearrange("q (g i) -> q g i", g=G),
                 in_=vec.rearrange("g (q i) o -> q g (i o)", i=32),
             )
-        xb_raw = load("xb_raw", x, HALF, N)
-        wo_raw = load("wo_raw", wo, 0, M)
-        dya_raw = load("dya_raw", dy, 0, HALF)
-        dyb_raw = load("dyb_raw", dy, HALF, N)
+        w2_raw = load("w2_raw", w2)
+        wo_raw = load("wo_raw", wo)
+        dy_raw = load("dy_raw", dy)
         base_sb = small("base_sb", G, N)
         nc.sync.dma_start(out=base_sb[:], in_=base.rearrange("g m n -> m g n"))
 
-        w12 = operand("w12", 2 * M)
-        wo_q = operand("wo_q", M)
-        xa, xb, dya, dyb = [operand(name, HALF) for name in ("xa", "xb", "dya", "dyb")]
-        z_ps = [[ps.tile([P, N], F32, name="z_ps%d%d" % (h, g)) for g in range(G)] for h in range(2)]
-        c_ps = [ps.tile([P, N], F32, name="c_ps%d" % g) for g in range(G)]
-        c_twin = [ps.tile([P, N], F32, name="c_twin%d" % g) for g in range(G)]
-        z_sb = [small("z_sb%d" % g, 2, N) for g in range(G)]
+        w1_q, w2_q, wo_q = [operand(name, M) for name in ("w1_q", "w2_q", "wo_q")]
+        x_q, dy_q = [operand(name, N) for name in ("x_q", "dy_q")]
+        z1_ps, z2_ps, c_ps = [
+            [ps.tile([P, N], F32, name="%s%d" % (name, g)) for g in range(G)] for name in ("z1", "z2", "c0")
+        ]
+        c_twin = ps.tile([P, N], F32, name="c0_twin")
+        z1 = [small("z1_sb%d" % g, N) for g in range(G)]
+        z2 = [small("z2_sb%d" % g, N) for g in range(G)]
         vcopy, scopy = nc.vector.tensor_copy, nc.scalar.copy
 
-        def z_out(copy, h, g):
-            copy(out=z_sb[g][:, :, h * HALF : (h + 1) * HALF], in_=z_ps[h][g][:].rearrange("p (k n) -> p k n", k=2))
-
-        interleave(vcopy, w12, 0, w1_raw, 0, M)
-        interleave(vcopy, w12, M, w2_raw, 0, M)
-        quantize(w12)
-
-        interleave(vcopy, xa, 0, xa_raw, 0, XA_V)
-        interleave(scopy, xa, 0, xa_raw, XA_V, HALF)
+        for lo in (0, HALF):
+            interleave(vcopy, x_q, x_raw, lo, lo + X_V)
+            interleave(scopy, x_q, x_raw, lo + X_V, lo + HALF)
+        interleave(scopy, w1_q, w1_raw, 0, M)
+        for lo in (0, HALF):
+            quantize(x_q, lo, lo + HALF)
+        quantize(w1_q, 0, M)
+        product(z1_ps, w1_q, x_q)
+        interleave(scopy, w2_q, w2_raw, 0, M)
         nc.vector.transpose(out=vec_cols[:], in_=vec_rows[:])
-        quantize(xa)
-        product(z_ps[0], 0, w12, 0, xa)
-        product(z_ps[0], HALF, w12, M, xa)
+        quantize(w2_q, 0, M)
+        product(z2_ps, w2_q, x_q)
+        interleave(scopy, wo_q, wo_raw, 0, M)
 
         t_st = small("t_st", G, 2)
         consts = small("consts", G, 3)
         gb_half = small("gb_half", G)
-        interleave(vcopy, xb, 0, xb_raw, 0, XB_V)
-        interleave(scopy, xb, 0, xb_raw, XB_V, HALF)
         fused(consts[:, :, 2], st_c, 0.5, ALU.mult, og_c)
         nc.vector.tensor_scalar(out=gb_half[:], in0=gb_c, scalar1=0.5, scalar2=None, op0=ALU.mult)
-        nc.vector.tensor_copy(out=consts[:, :, 0], in_=st_c)
+        nc.vector.tensor_scalar(out=consts[:, :, 0], in0=st_c, scalar1=0.5, scalar2=None, op0=ALU.mult)
         nc.vector.tensor_copy(out=t_st[:, :, 1], in_=st_c)
-        quantize(xb)
-        product(z_ps[1], 0, w12, 0, xb)
-        product(z_ps[1], HALF, w12, M, xb)
+        quantize(wo_q, 0, M)
 
-        interleave(scopy, wo_q, 0, wo_raw, 0, M)
-        z_out(vcopy, 0, 1)
-        z_out(scopy, 0, 0)
-        quantize(wo_q)
+        vcopy(out=z1[0][:], in_=z1_ps[0][:])
+        scopy(out=z1[1][:], in_=z1_ps[1][:])
 
-        interleave(vcopy, dya, 0, dya_raw, 0, DYA_V)
-        interleave(scopy, dya, 0, dya_raw, DYA_V, HALF)
-        quantize(dya)
-        product(c_ps, 0, wo_q, 0, dya)
-        product(c_twin, 0, wo_q, 0, dya)
-        z_out(scopy, 1, 0)
-
-        interleave(vcopy, dyb, 0, dyb_raw, 0, DYB_V)
-        interleave(scopy, dyb, 0, dyb_raw, DYB_V, HALF)
-        z_out(scopy, 1, 1)
-        quantize(dyb)
-        product(c_ps, HALF, wo_q, 0, dyb)
-        product(c_twin, HALF, wo_q, 0, dyb)
-
-        s12 = [cross_sum("s12_%d" % g, z_sb[g][:, 0, :], z_sb[g][:, 1, :], 0.5 / N) for g in range(G)]
-        s22 = [square_sum("s22_%d" % g, z_sb[g][:, 1, :]) for g in range(G)]
+        for lo in (0, HALF):
+            interleave(vcopy, dy_q, dy_raw, lo, lo + DY_V)
+            interleave(scopy, dy_q, dy_raw, lo + DY_V, lo + HALF)
+        for lo in (0, HALF):
+            quantize(dy_q, lo, lo + HALF)
+        product(c_ps, wo_q, dy_q)
+        product([c_twin], wo_q, dy_q)
+        for g in range(G):
+            scopy(out=z2[g][:], in_=z2_ps[g][:])
+        s12 = [cross_sum("s12_%d" % g, z2[g][:], z1[g][:], 0.5 / N) for g in range(G)]
+        s22 = [square_sum("s22_%d" % g, z2[g][:]) for g in range(G)]
+        coef = small("coef", G, 4)
         for g in range(G):
             nc.scalar.activation(
                 out=t_st[:, g, 0:1], in_=s12[g][:], func=ACT.Tanh, scale=t_st[:, g, 1:2], bias=gb_half[:, g : g + 1]
             )
         for g in range(G):
-            affine(consts[:, g, 1:2], s22[g][:], t_st[:, g, 1:2])
-        scc = [square_sum("scc_%d" % g, c_twin[g][:]) for g in range(G)]
+            affine(consts[:, g, 1:2], s22[g][:], consts[:, g, 0:1])
+        affine(coef[:, :, 0], t_st[:, :, 0], 1.0, 1.0)
+        scc_1 = square_sum("scc_1", c_ps[1][:])
+        scc = [square_sum("scc_0", c_twin[:]), scc_1]
 
         u_r = small("u_r", G, 2)
-        slopes = small("slopes", G, 3)
-        coef = small("coef", G, 3)
-        p0 = cross_sum("p0", c_ps[0][:], z_sb[0][:, 1, :], 0.5 / N)
+        p0 = cross_sum("p0", c_ps[0][:], z2[0][:], 0.5 / N)
         fused(u_r[:], t_st[:, :, 0:1].to_broadcast([P, G, 2]), -1.0, ALU.mult, t_st[:])
-        d0 = cross_sum("d0", c_ps[0][:], z_sb[0][:, 0, :], 1.0 / N)
-        fused(slopes[:], u_r[:, :, 0:1].to_broadcast([P, G, 3]), 1.0, ALU.add, consts[:])
-        p1 = cross_sum("p1", c_ps[1][:], z_sb[1][:, 1, :], 0.5 / N)
-        fused(coef[:, :, 0], t_st[:, :, 0], 1.0, ALU.add, slopes[:, :, 2])
-        fused(coef[:, :, 1:3], slopes[:, :, 0:2], 0.5, ALU.mult, slopes[:, :, 2:3].to_broadcast([P, G, 2]))
-        d1 = cross_sum("d1", c_ps[1][:], z_sb[1][:, 0, :], 1.0 / N)
+        d0 = cross_sum("d0", c_ps[0][:], z1[0][:], 1.0 / N)
+        fused(coef[:, :, 1:4], u_r[:, :, 0:1].to_broadcast([P, G, 3]), 1.0, ALU.add, consts[:])
+        p1 = cross_sum("p1", c_ps[1][:], z2[1][:], 0.5 / N)
+        d1 = cross_sum("d1", c_ps[1][:], z1[1][:], 1.0 / N)
         p_sum, d_sum = [p0, p1], [d0, d1]
 
         from_p = [small("from_p%d" % g, 2) for g in range(G)]
-        from_s = [small("from_s%d" % g, 1) for g in range(G)]
-        a_c = [small("a_c%d" % g, 1) for g in range(G)]
-        inner = [small("inner%d" % g, 1) for g in range(G)]
-        b_c = [small("b_c%d" % g, 1) for g in range(G)]
-        for g in range(G):
-            affine(from_p[g][:], coef[:, g, 0:2], p_sum[g][:])
-        affine(a_c[0][:], d_sum[0][:], coef[:, 0, 2:3], from_p[0][:, 0:1])
+        from_s, e_c, a_c, i_c, f_c, b_c = [
+            [small("%s%d" % (name, g), 1) for g in range(G)] for name in ("from_s", "e_c", "a_c", "i_c", "f_c", "b_c")
+        ]
+
+        def first_factor(g):
+            affine(e_c[g][:], d_sum[g][:], coef[:, g, 2:3], from_p[g][:, 0:1])
+
+        def both_factors(g):
+            affine(a_c[g][:], e_c[g][:], coef[:, g, 3:4])
+            affine(i_c[g][:], e_c[g][:], u_r[:, g, 1:2], from_p[g][:, 1:2])
+
+        def second_factor(g):
+            affine(f_c[g][:], i_c[g][:], d_sum[g][:], from_s[g][:])
+            affine(b_c[g][:], f_c[g][:], coef[:, g, 3:4])
+
+        affine(from_p[0][:], coef[:, 0, 0:2], p_sum[0][:])
+        first_factor(0)
         for g in range(G):
             affine(from_s[g][:], scc[g][:], coef[:, g, 0:1])
-        affine(inner[0][:], a_c[0][:], u_r[:, 0, 1:2], from_p[0][:, 1:2])
-        affine(a_c[1][:], d_sum[1][:], coef[:, 1, 2:3], from_p[1][:, 0:1])
-        affine(b_c[0][:], inner[0][:], d_sum[0][:], from_s[0][:])
-        affine(inner[1][:], a_c[1][:], u_r[:, 1, 1:2], from_p[1][:, 1:2])
-        affine(b_c[1][:], inner[1][:], d_sum[1][:], from_s[1][:])
+        both_factors(0)
+        affine(from_p[1][:], coef[:, 1, 0:2], p_sum[1][:])
+        second_factor(0)
+        first_factor(1)
+        both_factors(1)
+        second_factor(1)
 
-        part = [small("part%d" % g, N) for g in range(G)]
-        result = [small("result%d" % g, N) for g in range(G)]
         for g in range(G):
-            nc.vector.scalar_tensor_tensor(
-                out=part[g][:], in0=c_ps[g][:], scalar=a_c[g][:], in1=base_sb[:, g, :], op0=ALU.mult, op1=ALU.add
-            )
-        for g, cols in ((0, slice(0, N)), (1, slice(0, HALF)), (1, slice(HALF, N))):
-            nc.vector.scalar_tensor_tensor(
-                out=result[g][:, cols], in0=z_sb[g][:, 1, cols], scalar=b_c[g][:], in1=part[g][:, cols],
-                op0=ALU.mult, op1=ALU.add,
-            )
-            nc.sync.dma_start(out=out[g, :, cols], in_=result[g][:, cols])
+            part = small("part%d" % g, N)
+            result = small("result%d" % g, N)
+            for lo in (0, HALF):
+                cols = slice(lo, lo + HALF)
+                nc.vector.scalar_tensor_tensor(
+                    out=part[:, cols], in0=c_ps[g][:, cols], scalar=a_c[g][:], in1=base_sb[:, g, cols],
+                    op0=ALU.mult, op1=ALU.add,
+                )
+            for lo in (0, HALF):
+                cols = slice(lo, lo + HALF)
+                nc.vector.scalar_tensor_tensor(
+                    out=result[:, cols], in0=z2[g][:, cols], scalar=b_c[g][:], in1=part[:, cols],
+                    op0=ALU.mult, op1=ALU.add,
+                )
+                if g == G - 1:
+                    nc.sync.dma_start(out=out[g, :, cols], in_=result[:, cols])
+            if g < G - 1:
+                nc.sync.dma_start(out=out[g], in_=result[:])

@@ -19,7 +19,7 @@ ROWS = D // PACK
 HALF = N // 2
 RUN = 4
 X_V = 192
-DY_V = 176
+DY_V = 128
 
 
 def tile_rows_gprowgate_kernel(tc, x, w1, w2, st, gb, wo, dy, og, base, out):
@@ -56,18 +56,17 @@ def tile_rows_gprowgate_kernel(tc, x, w1, w2, st, gb, wo, dy, og, base, out):
                 in_=op[0][:, lo:hi, :].rearrange("p w j -> p (w j)"),
             )
 
-        def product(banks, weights, moving):
-            for g in range(len(banks)):
-                rows = slice(g * ROWS, (g + 1) * ROWS)
-                nc.tensor.matmul_mx(
-                    out=banks[g][:],
-                    lhsT=weights[1][rows, :].bitcast(FP8X4),
-                    lhsT_scale=weights[2][rows, :],
-                    rhs=moving[1][rows, :].bitcast(FP8X4),
-                    rhs_scale=moving[2][rows, :],
-                    start=True,
-                    stop=True,
-                )
+        def product(bank, g, weights, moving):
+            rows = slice(g * ROWS, (g + 1) * ROWS)
+            nc.tensor.matmul_mx(
+                out=bank[:],
+                lhsT=weights[1][rows, :].bitcast(FP8X4),
+                lhsT_scale=weights[2][rows, :],
+                rhs=moving[1][rows, :].bitcast(FP8X4),
+                rhs_scale=moving[2][rows, :],
+                start=True,
+                stop=True,
+            )
 
         def cross_sum(name, left, right, factor):
             total = small(name, 1)
@@ -77,10 +76,10 @@ def tile_rows_gprowgate_kernel(tc, x, w1, w2, st, gb, wo, dy, og, base, out):
             )
             return total
 
-        def square_sum(name, values):
+        def square_sum(name, values, divisor):
             total = small(name, 1)
             terms = small(name + "_terms", N)
-            nc.scalar.activation(out=terms[:], in_=values, func=ACT.Square, scale=1.0 / 32.0, accum_out=total[:])
+            nc.scalar.activation(out=terms[:], in_=values, func=ACT.Square, scale=divisor**-0.5, accum_out=total[:])
             return total
 
         def affine(result, value, scale, bias=0.0):
@@ -92,12 +91,11 @@ def tile_rows_gprowgate_kernel(tc, x, w1, w2, st, gb, wo, dy, og, base, out):
         vec_rows = sb.tile([P, P], F32, name="vec_rows", align_bytes=64)
         vec_cols = sb.tile([P, P], F32, name="vec_cols", align_bytes=64)
         nc.vector.memset(vec_rows[:], 0.0)
-        by_group = vec_cols[:].rearrange("p (g k) -> p g k", k=32)
-        st_c, gb_c, og_c = by_group[:, 0:G, 0], by_group[:, 0:G, 1], by_group[:, 0:G, 2]
+        row = vec_cols[:, 0 : G * 32].rearrange("p (g k) -> p g k", k=32)
 
         x_raw = load("x_raw", x)
         w1_raw = load("w1_raw", w1)
-        for k, vec in enumerate((st, gb, og)):
+        for k, vec in ((1, st), (5, gb), (6, og)):
             nc.sync.dma_start(
                 out=vec_rows[k:P:32, 0 : G * 32].rearrange("q (g i) -> q g i", g=G),
                 in_=vec.rearrange("g (q i) o -> q g (i o)", i=32),
@@ -125,82 +123,84 @@ def tile_rows_gprowgate_kernel(tc, x, w1, w2, st, gb, wo, dy, og, base, out):
         for lo in (0, HALF):
             quantize(x_q, lo, lo + HALF)
         quantize(w1_q, 0, M)
-        product(z1_ps, w1_q, x_q)
+        for g in range(G):
+            product(z1_ps[g], g, w1_q, x_q)
         interleave(scopy, w2_q, w2_raw, 0, M)
         nc.vector.transpose(out=vec_cols[:], in_=vec_rows[:])
         quantize(w2_q, 0, M)
-        product(z2_ps, w2_q, x_q)
+        for g in range(G):
+            product(z2_ps[g], g, w2_q, x_q)
         interleave(scopy, wo_q, wo_raw, 0, M)
-
-        t_st = small("t_st", G, 2)
-        consts = small("consts", G, 3)
-        gb_half = small("gb_half", G)
-        fused(consts[:, :, 2], st_c, 0.5, ALU.mult, og_c)
-        nc.vector.tensor_scalar(out=gb_half[:], in0=gb_c, scalar1=0.5, scalar2=None, op0=ALU.mult)
-        nc.vector.tensor_scalar(out=consts[:, :, 0], in0=st_c, scalar1=0.5, scalar2=None, op0=ALU.mult)
-        nc.vector.tensor_copy(out=t_st[:, :, 1], in_=st_c)
         quantize(wo_q, 0, M)
+        affine(row[:, :, 7], row[:, :, 5], 0.5)
+        affine(row[:, :, 2], row[:, :, 1], 0.5)
+        for g in range(G):
+            affine(row[:, g, 4:5], row[:, g, 6:7], row[:, g, 1:2])
 
         vcopy(out=z1[0][:], in_=z1_ps[0][:])
         scopy(out=z1[1][:], in_=z1_ps[1][:])
+        scopy(out=z2[0][:], in_=z2_ps[0][:])
 
-        for lo in (0, HALF):
-            interleave(vcopy, dy_q, dy_raw, lo, lo + DY_V)
-            interleave(scopy, dy_q, dy_raw, lo + DY_V, lo + HALF)
+        interleave(vcopy, dy_q, dy_raw, 0, HALF)
+        interleave(vcopy, dy_q, dy_raw, HALF, HALF + DY_V)
+        interleave(scopy, dy_q, dy_raw, HALF + DY_V, N)
         for lo in (0, HALF):
             quantize(dy_q, lo, lo + HALF)
-        product(c_ps, wo_q, dy_q)
-        product([c_twin], wo_q, dy_q)
         for g in range(G):
-            scopy(out=z2[g][:], in_=z2_ps[g][:])
+            product(c_ps[g], g, wo_q, dy_q)
+        product(c_twin, 0, wo_q, dy_q)
+        scopy(out=z2[1][:], in_=z2_ps[1][:])
         s12 = [cross_sum("s12_%d" % g, z2[g][:], z1[g][:], 0.5 / N) for g in range(G)]
-        s22 = [square_sum("s22_%d" % g, z2[g][:]) for g in range(G)]
-        coef = small("coef", G, 4)
+        s22 = [square_sum("s22_%d" % g, z2[g][:], 8 * N) for g in range(G)]
         for g in range(G):
+            affine(row[:, g, 3:4], s22[g][:], row[:, g, 1:2])
             nc.scalar.activation(
-                out=t_st[:, g, 0:1], in_=s12[g][:], func=ACT.Tanh, scale=t_st[:, g, 1:2], bias=gb_half[:, g : g + 1]
+                out=row[:, g, 0:1], in_=s12[g][:], func=ACT.Tanh, scale=row[:, g, 1:2], bias=row[:, g, 7:8]
             )
-        for g in range(G):
-            affine(consts[:, g, 1:2], s22[g][:], consts[:, g, 0:1])
-        affine(coef[:, :, 0], t_st[:, :, 0], 1.0, 1.0)
-        scc_1 = square_sum("scc_1", c_ps[1][:])
-        scc = [square_sum("scc_0", c_twin[:]), scc_1]
+        scc_1 = square_sum("scc_1", c_ps[1][:], 4 * N)
 
         u_r = small("u_r", G, 2)
-        p0 = cross_sum("p0", c_ps[0][:], z2[0][:], 0.5 / N)
-        fused(u_r[:], t_st[:, :, 0:1].to_broadcast([P, G, 2]), -1.0, ALU.mult, t_st[:])
+        coef = small("coef", G, 3)
+        p0 = cross_sum("p0", c_ps[0][:], z2[0][:], 0.25 / N)
+        fused(u_r[:], row[:, :, 0:1].to_broadcast([P, G, 2]), -1.0, ALU.mult, row[:, :, 0:2])
         d0 = cross_sum("d0", c_ps[0][:], z1[0][:], 1.0 / N)
-        fused(coef[:, :, 1:4], u_r[:, :, 0:1].to_broadcast([P, G, 3]), 1.0, ALU.add, consts[:])
-        p1 = cross_sum("p1", c_ps[1][:], z2[1][:], 0.5 / N)
+        fused(coef[:], u_r[:, :, 0:1].to_broadcast([P, G, 3]), 1.0, ALU.add, row[:, :, 2:5])
+        p1 = cross_sum("p1", c_ps[1][:], z2[1][:], 0.25 / N)
         d1 = cross_sum("d1", c_ps[1][:], z1[1][:], 1.0 / N)
         p_sum, d_sum = [p0, p1], [d0, d1]
 
-        from_p = [small("from_p%d" % g, 2) for g in range(G)]
-        from_s, e_c, a_c, i_c, f_c, b_c = [
-            [small("%s%d" % (name, g), 1) for g in range(G)] for name in ("from_s", "e_c", "a_c", "i_c", "f_c", "b_c")
+        p_gate, p_slope, s_gate, e_c, a_c, i_c, f_c, b_c = [
+            [small("%s%d" % (name, g), 1) for g in range(G)]
+            for name in ("p_gate", "p_slope", "s_gate", "e_c", "a_c", "i_c", "f_c", "b_c")
         ]
 
-        def first_factor(g):
-            affine(e_c[g][:], d_sum[g][:], coef[:, g, 2:3], from_p[g][:, 0:1])
+        def gated(result, total, g):
+            affine(result[:], total[:], row[:, g, 0:1], total[:])
 
-        def both_factors(g):
-            affine(a_c[g][:], e_c[g][:], coef[:, g, 3:4])
-            affine(i_c[g][:], e_c[g][:], u_r[:, g, 1:2], from_p[g][:, 1:2])
+        def first_step(g):
+            affine(e_c[g][:], d_sum[g][:], coef[:, g, 1:2], p_gate[g][:])
 
-        def second_factor(g):
-            affine(f_c[g][:], i_c[g][:], d_sum[g][:], from_s[g][:])
-            affine(b_c[g][:], f_c[g][:], coef[:, g, 3:4])
+        def second_step(g):
+            affine(a_c[g][:], e_c[g][:], coef[:, g, 2:3])
+            affine(i_c[g][:], e_c[g][:], u_r[:, g, 1:2], p_slope[g][:])
 
-        affine(from_p[0][:], coef[:, 0, 0:2], p_sum[0][:])
-        first_factor(0)
-        for g in range(G):
-            affine(from_s[g][:], scc[g][:], coef[:, g, 0:1])
-        both_factors(0)
-        affine(from_p[1][:], coef[:, 1, 0:2], p_sum[1][:])
-        second_factor(0)
-        first_factor(1)
-        both_factors(1)
-        second_factor(1)
+        def last_steps(g):
+            affine(f_c[g][:], i_c[g][:], d_sum[g][:], s_gate[g][:])
+            affine(b_c[g][:], f_c[g][:], coef[:, g, 2:3])
+
+        gated(p_gate[0], p0, 0)
+        scc_0 = square_sum("scc_0", c_twin[:], 4 * N)
+        first_step(0)
+        affine(p_slope[0][:], p0[:], coef[:, 0, 0:1])
+        gated(s_gate[1], scc_1, 1)
+        gated(s_gate[0], scc_0, 0)
+        second_step(0)
+        gated(p_gate[1], p1, 1)
+        affine(p_slope[1][:], p1[:], coef[:, 1, 0:1])
+        last_steps(0)
+        first_step(1)
+        second_step(1)
+        last_steps(1)
 
         for g in range(G):
             part = small("part%d" % g, N)

@@ -19,7 +19,7 @@ ROWS = D // PACK
 HALF = N // 2
 RUN = 4
 X_V = 192
-DY_V = 128
+DY_V = 112
 
 
 def tile_rows_gprowgate_kernel(tc, x, w1, w2, st, gb, wo, dy, og, base, out):
@@ -101,8 +101,8 @@ def tile_rows_gprowgate_kernel(tc, x, w1, w2, st, gb, wo, dy, og, base, out):
                 in_=vec.rearrange("g (q i) o -> q g (i o)", i=32),
             )
         w2_raw = load("w2_raw", w2)
-        wo_raw = load("wo_raw", wo)
         dy_raw = load("dy_raw", dy)
+        wo_raw = load("wo_raw", wo)
         base_sb = small("base_sb", G, N)
         nc.sync.dma_start(out=base_sb[:], in_=base.rearrange("g m n -> m g n"))
 
@@ -130,8 +130,6 @@ def tile_rows_gprowgate_kernel(tc, x, w1, w2, st, gb, wo, dy, og, base, out):
         quantize(w2_q, 0, M)
         for g in range(G):
             product(z2_ps[g], g, w2_q, x_q)
-        interleave(scopy, wo_q, wo_raw, 0, M)
-        quantize(wo_q, 0, M)
         affine(row[:, :, 7], row[:, :, 5], 0.5)
         affine(row[:, :, 2], row[:, :, 1], 0.5)
         for g in range(G):
@@ -139,17 +137,19 @@ def tile_rows_gprowgate_kernel(tc, x, w1, w2, st, gb, wo, dy, og, base, out):
 
         vcopy(out=z1[0][:], in_=z1_ps[0][:])
         scopy(out=z1[1][:], in_=z1_ps[1][:])
-        scopy(out=z2[0][:], in_=z2_ps[0][:])
 
         interleave(vcopy, dy_q, dy_raw, 0, HALF)
         interleave(vcopy, dy_q, dy_raw, HALF, HALF + DY_V)
         interleave(scopy, dy_q, dy_raw, HALF + DY_V, N)
+        interleave(vcopy, wo_q, wo_raw, 0, M)
         for lo in (0, HALF):
             quantize(dy_q, lo, lo + HALF)
+        quantize(wo_q, 0, M)
         for g in range(G):
             product(c_ps[g], g, wo_q, dy_q)
         product(c_twin, 0, wo_q, dy_q)
-        scopy(out=z2[1][:], in_=z2_ps[1][:])
+        for g in range(G):
+            scopy(out=z2[g][:], in_=z2_ps[g][:])
         s12 = [cross_sum("s12_%d" % g, z2[g][:], z1[g][:], 0.5 / N) for g in range(G)]
         s22 = [square_sum("s22_%d" % g, z2[g][:], 8 * N) for g in range(G)]
         for g in range(G):
@@ -195,6 +195,11 @@ def tile_rows_gprowgate_kernel(tc, x, w1, w2, st, gb, wo, dy, og, base, out):
         gated(s_gate[1], scc_1, 1)
         gated(s_gate[0], scc_0, 0)
         second_step(0)
+        left, right = slice(0, HALF), slice(HALF, N)
+        scaled = small("scaled", HALF)
+        part = {(g, lo): small("part%d_%d" % (g, lo), HALF) for g in range(G) for lo in (0, HALF)}
+        affine(scaled[:], c_twin[:, left], a_c[0][:])
+        nc.gpsimd.tensor_tensor(out=part[0, 0][:], in0=scaled[:], in1=base_sb[:, 0, left], op=ALU.add)
         gated(p_gate[1], p1, 1)
         affine(p_slope[1][:], p1[:], coef[:, 1, 0:1])
         last_steps(0)
@@ -202,22 +207,24 @@ def tile_rows_gprowgate_kernel(tc, x, w1, w2, st, gb, wo, dy, og, base, out):
         second_step(1)
         last_steps(1)
 
-        for g in range(G):
-            part = small("part%d" % g, N)
-            result = small("result%d" % g, N)
-            for lo in (0, HALF):
-                cols = slice(lo, lo + HALF)
-                nc.vector.scalar_tensor_tensor(
-                    out=part[:, cols], in0=c_ps[g][:, cols], scalar=a_c[g][:], in1=base_sb[:, g, cols],
-                    op0=ALU.mult, op1=ALU.add,
-                )
-            for lo in (0, HALF):
-                cols = slice(lo, lo + HALF)
-                nc.vector.scalar_tensor_tensor(
-                    out=result[:, cols], in0=z2[g][:, cols], scalar=b_c[g][:], in1=part[:, cols],
-                    op0=ALU.mult, op1=ALU.add,
-                )
-                if g == G - 1:
-                    nc.sync.dma_start(out=out[g, :, cols], in_=result[:, cols])
-            if g < G - 1:
-                nc.sync.dma_start(out=out[g], in_=result[:])
+        def add_c0(g, cols):
+            nc.vector.scalar_tensor_tensor(
+                out=part[g, cols.start][:], in0=c_ps[g][:, cols], scalar=a_c[g][:], in1=base_sb[:, g, cols],
+                op0=ALU.mult, op1=ALU.add,
+            )
+
+        def add_z2_and_store(g, cols):
+            result = small("result%d_%d" % (g, cols.start), HALF)
+            nc.vector.scalar_tensor_tensor(
+                out=result[:], in0=z2_ps[g][:, cols], scalar=b_c[g][:], in1=part[g, cols.start][:],
+                op0=ALU.mult, op1=ALU.add,
+            )
+            nc.sync.dma_start(out=out[g, :, cols], in_=result[:])
+
+        add_c0(0, right)
+        add_z2_and_store(0, right)
+        add_c0(1, left)
+        add_z2_and_store(0, left)
+        add_c0(1, right)
+        add_z2_and_store(1, left)
+        add_z2_and_store(1, right)

from contextlib import ExitStack

import concourse.mybir as mybir

G, D, M, N = 2, 256, 128, 512
FLOPS = 3 * 2 * G * D * M * N

F32 = mybir.dt.float32
BF16 = mybir.dt.bfloat16
U32 = mybir.dt.uint32
U8 = mybir.dt.uint8
FP8X4 = mybir.dt.float8_e4m3fn_x4
ALU = mybir.AluOpType
ACT = mybir.ActivationFunctionType

P = 128
PACK = 4
ROWS = D // PACK
HALF = N // 2
RUN = 4
X_V = 192
DY_V = 112


def tile_rows_gprowgate_kernel(tc, x, w1, w2, st, gb, wo, dy, og, base, out):
    nc = tc.nc
    with ExitStack() as ctx:
        sb = ctx.enter_context(tc.tile_pool(name="sb", bufs=1))
        ps = ctx.enter_context(tc.psum_pool(name="ps", bufs=1))
        ctx.enter_context(tc.manual_schedule())

        def small(name, *shape):
            return sb.tile([P, *shape], F32, name=name)

        def load(name, src):
            raw = sb.tile([P, PACK, src.shape[2]], F32, name=name, align_bytes=64)
            nc.sync.dma_start(out=raw[:], in_=src.rearrange("g (p j) n -> (g p) j n", j=PACK))
            return raw

        def operand(name, width):
            grouped = sb.tile([P, width, PACK], BF16, name=name + "_bf", align_bytes=64)
            codes = sb.tile([P, width], U32, name=name + "_codes", align_bytes=64)
            scales = sb.tile([P, width], U8, name=name + "_scales", align_bytes=64)
            return grouped, codes, scales

        def interleave(copy, op, raw, lo, hi):
            copy(
                out=op[0][:, lo:hi, :].rearrange("p (c i) j -> p c j i", i=RUN),
                in_=raw[:, :, lo:hi].rearrange("p j (c i) -> p c j i", i=RUN),
            )

        def quantize(op, lo, hi):
            nc.vector.quantize_mx(
                out=op[1][:, lo:hi].bitcast(FP8X4),
                scales=op[2][:, lo:hi],
                in_=op[0][:, lo:hi, :].rearrange("p w j -> p (w j)"),
            )

        def product(bank, g, weights, moving):
            rows = slice(g * ROWS, (g + 1) * ROWS)
            nc.tensor.matmul_mx(
                out=bank[:],
                lhsT=weights[1][rows, :].bitcast(FP8X4),
                lhsT_scale=weights[2][rows, :],
                rhs=moving[1][rows, :].bitcast(FP8X4),
                rhs_scale=moving[2][rows, :],
                start=True,
                stop=True,
            )

        def cross_sum(name, left, right, factor):
            total = small(name, 1)
            terms = small(name + "_terms", N)
            nc.vector.scalar_tensor_tensor(
                out=terms[:], in0=left, scalar=factor, in1=right, op0=ALU.mult, op1=ALU.mult, accum_out=total[:]
            )
            return total

        def square_sum(name, values, divisor):
            total = small(name, 1)
            terms = small(name + "_terms", N)
            nc.scalar.activation(out=terms[:], in_=values, func=ACT.Square, scale=divisor**-0.5, accum_out=total[:])
            return total

        def affine(result, value, scale, bias=0.0):
            nc.scalar.activation(out=result, in_=value, func=ACT.Identity, scale=scale, bias=bias)

        def fused(result, in0, number, op0, in1):
            nc.vector.scalar_tensor_tensor(out=result, in0=in0, scalar=number, in1=in1, op0=op0, op1=ALU.mult)

        vec_rows = sb.tile([P, P], F32, name="vec_rows", align_bytes=64)
        vec_cols = sb.tile([P, P], F32, name="vec_cols", align_bytes=64)
        nc.vector.memset(vec_rows[:], 0.0)
        row = vec_cols[:, 0 : G * 32].rearrange("p (g k) -> p g k", k=32)

        x_raw = load("x_raw", x)
        w1_raw = load("w1_raw", w1)
        for k, vec in ((1, st), (5, gb), (6, og)):
            nc.sync.dma_start(
                out=vec_rows[k:P:32, 0 : G * 32].rearrange("q (g i) -> q g i", g=G),
                in_=vec.rearrange("g (q i) o -> q g (i o)", i=32),
            )
        w2_raw = load("w2_raw", w2)
        dy_raw = load("dy_raw", dy)
        wo_raw = load("wo_raw", wo)
        base_sb = small("base_sb", G, N)
        nc.sync.dma_start(out=base_sb[:], in_=base.rearrange("g m n -> m g n"))

        w1_q, w2_q, wo_q = [operand(name, M) for name in ("w1_q", "w2_q", "wo_q")]
        x_q, dy_q = [operand(name, N) for name in ("x_q", "dy_q")]
        z1_ps, z2_ps, c_ps = [
            [ps.tile([P, N], F32, name="%s%d" % (name, g)) for g in range(G)] for name in ("z1", "z2", "c0")
        ]
        c_twin = ps.tile([P, N], F32, name="c0_twin")
        z1 = [small("z1_sb%d" % g, N) for g in range(G)]
        z2 = [small("z2_sb%d" % g, N) for g in range(G)]
        vcopy, scopy = nc.vector.tensor_copy, nc.scalar.copy

        for lo in (0, HALF):
            interleave(vcopy, x_q, x_raw, lo, lo + X_V)
            interleave(scopy, x_q, x_raw, lo + X_V, lo + HALF)
        interleave(scopy, w1_q, w1_raw, 0, M)
        for lo in (0, HALF):
            quantize(x_q, lo, lo + HALF)
        quantize(w1_q, 0, M)
        for g in range(G):
            product(z1_ps[g], g, w1_q, x_q)
        interleave(scopy, w2_q, w2_raw, 0, M)
        nc.vector.transpose(out=vec_cols[:], in_=vec_rows[:])
        quantize(w2_q, 0, M)
        for g in range(G):
            product(z2_ps[g], g, w2_q, x_q)
        affine(row[:, :, 7], row[:, :, 5], 0.5)
        affine(row[:, :, 2], row[:, :, 1], 0.5)
        for g in range(G):
            affine(row[:, g, 4:5], row[:, g, 6:7], row[:, g, 1:2])

        vcopy(out=z1[0][:], in_=z1_ps[0][:])
        scopy(out=z1[1][:], in_=z1_ps[1][:])

        interleave(vcopy, dy_q, dy_raw, 0, HALF)
        interleave(vcopy, dy_q, dy_raw, HALF, HALF + DY_V)
        interleave(scopy, dy_q, dy_raw, HALF + DY_V, N)
        interleave(vcopy, wo_q, wo_raw, 0, M)
        for lo in (0, HALF):
            quantize(dy_q, lo, lo + HALF)
        quantize(wo_q, 0, M)
        for g in range(G):
            product(c_ps[g], g, wo_q, dy_q)
        product(c_twin, 0, wo_q, dy_q)
        for g in range(G):
            scopy(out=z2[g][:], in_=z2_ps[g][:])
        s12 = [cross_sum("s12_%d" % g, z2[g][:], z1[g][:], 0.5 / N) for g in range(G)]
        s22 = [square_sum("s22_%d" % g, z2[g][:], 8 * N) for g in range(G)]
        for g in range(G):
            affine(row[:, g, 3:4], s22[g][:], row[:, g, 1:2])
            nc.scalar.activation(
                out=row[:, g, 0:1], in_=s12[g][:], func=ACT.Tanh, scale=row[:, g, 1:2], bias=row[:, g, 7:8]
            )
        scc_1 = square_sum("scc_1", c_ps[1][:], 4 * N)

        u_r = small("u_r", G, 2)
        coef = small("coef", G, 3)
        p0 = cross_sum("p0", c_ps[0][:], z2[0][:], 0.25 / N)
        fused(u_r[:], row[:, :, 0:1].to_broadcast([P, G, 2]), -1.0, ALU.mult, row[:, :, 0:2])
        d0 = cross_sum("d0", c_ps[0][:], z1[0][:], 1.0 / N)
        fused(coef[:], u_r[:, :, 0:1].to_broadcast([P, G, 3]), 1.0, ALU.add, row[:, :, 2:5])
        p1 = cross_sum("p1", c_ps[1][:], z2[1][:], 0.25 / N)
        d1 = cross_sum("d1", c_ps[1][:], z1[1][:], 1.0 / N)
        p_sum, d_sum = [p0, p1], [d0, d1]

        p_gate, p_slope, s_gate, e_c, a_c, i_c, f_c, b_c = [
            [small("%s%d" % (name, g), 1) for g in range(G)]
            for name in ("p_gate", "p_slope", "s_gate", "e_c", "a_c", "i_c", "f_c", "b_c")
        ]

        def gated(result, total, g):
            affine(result[:], total[:], row[:, g, 0:1], total[:])

        def first_step(g):
            affine(e_c[g][:], d_sum[g][:], coef[:, g, 1:2], p_gate[g][:])

        def second_step(g):
            affine(a_c[g][:], e_c[g][:], coef[:, g, 2:3])
            affine(i_c[g][:], e_c[g][:], u_r[:, g, 1:2], p_slope[g][:])

        def last_steps(g):
            affine(f_c[g][:], i_c[g][:], d_sum[g][:], s_gate[g][:])
            affine(b_c[g][:], f_c[g][:], coef[:, g, 2:3])

        gated(p_gate[0], p0, 0)
        scc_0 = square_sum("scc_0", c_twin[:], 4 * N)
        first_step(0)
        affine(p_slope[0][:], p0[:], coef[:, 0, 0:1])
        gated(s_gate[1], scc_1, 1)
        gated(s_gate[0], scc_0, 0)
        second_step(0)
        left, right = slice(0, HALF), slice(HALF, N)
        scaled = small("scaled", HALF)
        part = {(g, lo): small("part%d_%d" % (g, lo), HALF) for g in range(G) for lo in (0, HALF)}
        affine(scaled[:], c_twin[:, left], a_c[0][:])
        nc.gpsimd.tensor_tensor(out=part[0, 0][:], in0=scaled[:], in1=base_sb[:, 0, left], op=ALU.add)
        gated(p_gate[1], p1, 1)
        affine(p_slope[1][:], p1[:], coef[:, 1, 0:1])
        last_steps(0)
        first_step(1)
        second_step(1)
        last_steps(1)

        def add_c0(g, cols):
            nc.vector.scalar_tensor_tensor(
                out=part[g, cols.start][:], in0=c_ps[g][:, cols], scalar=a_c[g][:], in1=base_sb[:, g, cols],
                op0=ALU.mult, op1=ALU.add,
            )

        def add_z2_and_store(g, cols):
            result = small("result%d_%d" % (g, cols.start), HALF)
            nc.vector.scalar_tensor_tensor(
                out=result[:], in0=z2_ps[g][:, cols], scalar=b_c[g][:], in1=part[g, cols.start][:],
                op0=ALU.mult, op1=ALU.add,
            )
            nc.sync.dma_start(out=out[g, :, cols], in_=result[:])

        add_c0(0, right)
        add_z2_and_store(0, right)
        add_c0(1, left)
        add_z2_and_store(0, left)
        add_c0(1, right)
        add_z2_and_store(1, left)
        add_z2_and_store(1, right)
